import numpy as np
import ml_dtypes


def mxq(x, axis, fmt="e4m3"):
    dtype, down = {"e4m3": (ml_dtypes.float8_e4m3fn, 7), "e5m2": (ml_dtypes.float8_e5m2, 14)}[fmt]
    v = np.moveaxis(np.asarray(x, np.float32).astype(ml_dtypes.bfloat16).astype(np.float64), axis, -1)
    blocks = v.reshape(v.shape[:-1] + (-1, 32))
    amax = np.abs(blocks).max(-1, keepdims=True)
    byte = np.maximum(np.where(amax > 0, np.frexp(amax)[1] - 1 + 127, 0) - down, 1)
    scale = np.exp2(byte - 127.0)
    codes = (blocks / scale).astype(np.float32).astype(dtype).astype(np.float64)
    return np.moveaxis((codes * scale).reshape(v.shape), -1, axis)


WIDE = False


def mx_kscale(k):
    if not WIDE:
        return np.ones(k)
    levels = np.array([10, -10, 5, -5, 0])
    if k % 512:
        return np.exp2(np.random.permutation(np.resize(levels, k // 32))).repeat(32)
    a = np.empty((k // 512, 16))
    for p in range(k // 512):
        a[p, :8] = np.random.permutation(np.resize(levels, 8))
        for g in range(8):
            far = levels[np.abs(levels - a[p, g]) >= 10]
            a[p, g + 8] = far[np.random.randint(len(far))]
    return np.exp2(a.ravel()).repeat(32)


def f64(x):
    return np.asarray(x).astype(np.float64)


def striped(idx):
    return np.tile(np.asarray(idx).reshape(-1, 16).T, (8, 1)).astype(np.uint16)


def unstriped(offs):
    return offs[:16].T.reshape(-1).astype(np.int64)


E2M1 = np.array([0.0, 0.5, 1.0, 1.5, 2.0, 3.0, 4.0, 6.0, -0.0, -0.5, -1.0, -1.5, -2.0, -3.0, -4.0, -6.0])


def pack_weight(w, fmt):
    k, n = w.shape
    w = f64(np.asarray(w, np.float32).astype(ml_dtypes.bfloat16)).reshape(k // 32, 32, n)
    amax = np.abs(w).max(1)
    if fmt == "e4m3":
        byte = np.frexp(amax)[1] - 1 + 127 - 7
    else:
        mant, ex = np.frexp(amax / 6.0)
        byte = np.where(mant > 0.5, ex, ex - 1) + 127
    byte = np.clip(np.where(amax > 0, byte, 1), 1, 254)
    scaled = (w * np.exp2(127.0 - byte)[:, None, :]).reshape(k, n).astype(np.float32)
    by_word = np.ascontiguousarray(scaled.reshape(k // 512, 128, 4, n).transpose(0, 1, 3, 2))
    if fmt == "e4m3":
        words = by_word.astype(ml_dtypes.float8_e4m3fn).view(np.uint8)
    else:
        c = by_word.astype(ml_dtypes.float4_e2m1fn).view(np.uint8) & 0xF
        words = (c[..., 0::2] | (c[..., 1::2] << 4)).reshape(k // 512, 128, 2 * n)
    return np.ascontiguousarray(words), np.ascontiguousarray(byte.astype(np.uint8).reshape(k // 512, 16, n))


def unpack_weight(words, scales, fmt):
    g, _, n = scales.shape
    words = np.ascontiguousarray(words).reshape(g, 128, n, -1)
    if fmt == "e4m3":
        vals = words.view(ml_dtypes.float8_e4m3fn).astype(np.float64)
    else:
        nib = np.empty((g, 128, n, 4), np.uint8)
        nib[..., 0::2] = words & 0xF
        nib[..., 1::2] = words >> 4
        vals = E2M1[nib]
    vals = vals * np.repeat(np.exp2(scales.astype(np.float64) - 127.0), 8, axis=1)[..., None]
    return vals.transpose(0, 1, 3, 2).reshape(g * 512, n)


def sigmoid(v):
    return 1.0 / (1.0 + np.exp(-v))


def bf(x):
    return np.asarray(x, np.float32).astype(ml_dtypes.bfloat16)


def planes(Y):
    r, m = Y.shape
    b = f64(bf(Y)).reshape(r // 32, 32, m)
    amax = np.abs(b).max(1)
    byte = np.clip(np.where(amax > 0, np.frexp(amax)[1] - 1 + 127 - 7, 1), 1, 254)
    codes = (b * np.exp2(127.0 - byte)[:, None, :]).reshape(r, m).astype(np.float32).astype(ml_dtypes.float8_e4m3fn).view(np.uint8)
    words = codes.reshape(r // 512, 128, 4, m).transpose(0, 1, 3, 2)
    return np.ascontiguousarray(words), np.ascontiguousarray(byte.astype(np.uint8).reshape(r // 512, 16, m))


B, N, T, D, NQ = 1, 512, 2048, 512, 512


def setup_inputs():
    n = np.random.standard_normal
    idx = np.random.permutation(T)[:B * N]
    s = mx_kscale(D)[:, None]
    mid = n((D, T))
    kp = pack_weight((mid + np.abs(n((D, T)))) / s, "e4m3")
    cp = pack_weight((mid - np.abs(n((D, T)))) / s, "e4m3")
    return {
        "qT": (n((B, D, NQ)) * s * (1.00 / np.sqrt(D))).astype(np.float32),
        "k_words": kp[0],
        "k_scales": kp[1],
        "c_words": cp[0],
        "c_scales": cp[1],
        "th": (14 + 2 * n((B, 1, NQ))).astype(np.float32),
        "offs": striped(idx),
    }


def reference(qT, k_words, k_scales, c_words, c_scales, th, offs):
    idx = unstriped(offs)
    pick = lambda x, which: x[:, which].reshape(x.shape[0], B, -1).transpose(1, 0, 2)
    k = unpack_weight(k_words, k_scales, "e4m3")
    kg = pick(k, idx)
    c = unpack_weight(c_words, c_scales, "e4m3")
    cg = pick(c, idx)
    hiq = mxq(np.maximum(f64(qT), 0.0), 1, "e4m3")
    loq = mxq(np.minimum(f64(qT), 0.0), 1, "e4m3")
    a = (kg.transpose(0, 2, 1) @ hiq) + (cg.transpose(0, 2, 1) @ loq)
    y = sigmoid(a - f64(th))
    Y = y[0]
    words, scales = planes(Y)
    return Y, words, scales

@@ -1,0 +1,155 @@
+from contextlib import ExitStack
+
+import concourse.mybir as mybir
+from concourse.masks import make_identity
+
+F32 = mybir.dt.float32
+BF16 = mybir.dt.bfloat16
+I32 = mybir.dt.int32
+U32 = mybir.dt.uint32
+U16 = mybir.dt.uint16
+U8 = mybir.dt.uint8
+FP8X4 = mybir.dt.float8_e4m3fn_x4
+ALU = mybir.AluOpType
+ACT = mybir.ActivationFunctionType
+
+P = 128
+PACK = 4
+PAGES = 2048
+SLOTS = 512
+NQ = 512
+HALVES = 2
+HALF = NQ // HALVES
+FLOPS = 2 * 2 * SLOTS * 512 * NQ
+
+
+def interleaved(dst):
+    return dst.rearrange("p (c i) t -> p c t i", i=4)
+
+
+def by_rows(src):
+    return src.rearrange("p t (c i) -> p c t i", i=4)
+
+
+def tile_attend_plw_quest_topk_kernel(tc, qT, k_words, k_scales, c_words, c_scales, th, offs, out_0, out_1, out_2):
+    nc = tc.nc
+    with ExitStack() as ctx:
+        keep = ctx.enter_context(tc.tile_pool(name="keep", bufs=1))
+        psum = ctx.enter_context(tc.psum_pool(name="psum", bufs=1))
+
+        offsets = keep.tile([P, SLOTS // 16], U16, name="offsets")
+        nc.sync.dma_start(offsets[:], offs)
+
+        ks_pool = keep.tile([P, PAGES], U8, name="ks_pool")
+        cs_pool = keep.tile([P, PAGES], U8, name="cs_pool")
+        nc.vector.memset(ks_pool[:].bitcast(I32), 0)
+        nc.vector.memset(cs_pool[:].bitcast(I32), 0)
+        for quad in range(4):
+            nc.scalar.dma_start(ks_pool[32 * quad : 32 * quad + 4, :].bitcast(I32), k_scales[0, 4 * quad : 4 * quad + 4, :].bitcast(I32))
+        for quad in range(4):
+            nc.gpsimd.dma_start(cs_pool[32 * quad : 32 * quad + 4, :].bitcast(I32), c_scales[0, 4 * quad : 4 * quad + 4, :].bitcast(I32))
+        th_cols = keep.tile([P, PACK], F32, name="th_cols")
+        nc.gpsimd.dma_start(th_cols[:], th[0, 0, :].rearrange("(p c) -> p c", c=PACK))
+
+        warm_in = keep.tile([P, 1], F32, name="warm_in")
+        warm_out = keep.tile([P, 1], F32, name="warm_out")
+        nc.vector.memset(warm_in[:], 0.0)
+        nc.scalar.activation(warm_out[:], warm_in[:], ACT.Sigmoid)
+
+        q_rows = qT[0].rearrange("(p t) q -> p t q", t=PACK)
+        q_raw = []
+        for h in range(HALVES):
+            raw = keep.tile([P, PACK, HALF], F32, name=f"q_raw{h}", tag=f"stage{h}")
+            nc.sync.dma_start(raw[:], q_rows[:, :, h * HALF : (h + 1) * HALF])
+            q_raw.append(raw)
+        k_pool = keep.tile([P, PAGES], I32, name="k_pool")
+        nc.sync.dma_start(k_pool[:], k_words[0].rearrange("p n t -> p (n t)").bitcast(I32))
+
+        def gather_scales(pool, name):
+            listed = keep.tile([P, SLOTS], U8, name=name + "_listed", tag=name + "_chain", align_bytes=64)
+            dealt = keep.tile([P, SLOTS], U8, name=name + "_dealt", align_bytes=64)
+            nc.vector.tensor_copy(listed[:], pool[:].indirect(offsets[:]))
+            nc.vector.tensor_copy(dealt[:].rearrange("p (t s) -> p t s", t=PACK), listed[:].rearrange("p (s t) -> p t s", t=PACK))
+            return dealt
+
+        def gather_words(pool, name, tag):
+            dealt = keep.tile([P, SLOTS], U32, name=name, tag=tag, align_bytes=64)
+            nc.vector.tensor_copy(dealt[:].rearrange("p (t s) -> p s t", t=PACK), pool[:].bitcast(U32).indirect(offsets[:]))
+            return dealt
+
+        def quantize(values, codes, scales):
+            nc.vector.quantize_mx(out=codes.bitcast(FP8X4), scales=scales, in_=values.rearrange("p c t -> p (c t)"))
+
+        ks = gather_scales(ks_pool, "ks")
+        cs = gather_scales(cs_pool, "cs")
+
+        q_bf = [keep.tile([P, HALF, PACK], BF16, name=f"q_bf{h}", align_bytes=64) for h in range(HALVES)]
+        hi = [keep.tile([P, HALF, PACK], BF16, name=f"hi{h}", tag=("hi0", "cs_chain")[h], align_bytes=64) for h in range(HALVES)]
+        lo = [keep.tile([P, HALF, PACK], BF16, name=f"lo{h}", align_bytes=64) for h in range(HALVES)]
+        hi_codes = [keep.tile([P, HALF], U32, name=f"hi_codes{h}", align_bytes=64) for h in range(HALVES)]
+        lo_codes = [keep.tile([P, HALF], U32, name=f"lo_codes{h}", align_bytes=64) for h in range(HALVES)]
+        hi_scales = [keep.tile([P, HALF], U8, name=f"hi_scales{h}", align_bytes=64) for h in range(HALVES)]
+        lo_scales = [keep.tile([P, HALF], U8, name=f"lo_scales{h}", align_bytes=64) for h in range(HALVES)]
+        for h in range(HALVES):
+            nc.scalar.copy(interleaved(q_bf[h][:]), by_rows(q_raw[h][:]))
+        c_pool = keep.tile([P, PAGES], I32, name="c_pool", tag="stage0")
+        nc.sync.dma_start(c_pool[:], c_words[0].rearrange("p n t -> p (n t)").bitcast(I32))
+        nc.scalar.activation(hi[0][:], q_bf[0][:], ACT.Relu)
+        nc.vector.tensor_scalar_min(lo[0][:], q_bf[0][:], 0.0)
+        nc.vector.tensor_scalar_max(hi[1][:], q_bf[1][:], 0.0)
+        nc.vector.tensor_scalar_min(lo[1][:], q_bf[1][:], 0.0)
+        quantize(lo[0][:], lo_codes[0][:], lo_scales[0][:])
+        quantize(hi[1][:], hi_codes[1][:], hi_scales[1][:])
+        quantize(hi[0][:], hi_codes[0][:], hi_scales[0][:])
+        kw = gather_words(k_pool, "kw", "cs_chain")
+        quantize(lo[1][:], lo_codes[1][:], lo_scales[1][:])
+        cw = gather_words(c_pool, "cw", "cw")
+
+        ident = keep.tile([P, P], F32, name="ident")
+        make_identity(nc, ident[:])
+        th_bank = psum.tile([P, PACK, P], F32, name="th_bank", tag="bank7")
+        for c in range(PACK):
+            nc.tensor.transpose(th_bank[:, c, :], th_cols[:, c : c + 1].to_broadcast([P, P]), ident[:])
+        th_rows = keep.tile([P, NQ], F32, name="th_rows")
+        nc.scalar.copy(th_rows[:].rearrange("p (n c) -> p n c", c=PACK), th_bank[:].rearrange("p c n -> p n c"))
+
+        banks = [[psum.tile([P, HALF], F32, name=f"acc{h}{u}", tag=f"bank{PACK * h + u}") for u in range(PACK)] for h in range(HALVES)]
+
+        def product(words, scales, codes, q_scales, first):
+            for h in range(HALVES):
+                for u in range(PACK):
+                    cols = slice(u * P, (u + 1) * P)
+                    nc.tensor.matmul_mx(
+                        out=banks[h][u][:],
+                        lhsT=words[:, cols].bitcast(FP8X4),
+                        lhsT_scale=scales[:, cols],
+                        rhs=codes[h][:].bitcast(FP8X4),
+                        rhs_scale=q_scales[h][:],
+                        start=first,
+                        stop=not first,
+                    )
+
+        product(kw, ks, hi_codes, hi_scales, True)
+        product(cw, cs, lo_codes, lo_scales, False)
+
+        y_rows = out_0.rearrange("(p u) q -> p u q", u=PACK)
+        word_rows = out_1[0].rearrange("p q t -> p (q t)").bitcast(I32)
+        y_scales = keep.tile([P, NQ], U8, name="y_scales", align_bytes=64)
+        z = [keep.tile([P, PACK, HALF], F32, name=f"z{h}") for h in range(HALVES)]
+        y = [keep.tile([P, PACK, HALF], F32, name=f"y{h}") for h in range(HALVES)]
+        for h in range(HALVES):
+            cols = slice(h * HALF, (h + 1) * HALF)
+            for u in range(PACK):
+                nc.vector.tensor_sub(z[h][:, u, :], banks[h][u][:], th_rows[:, cols])
+                nc.scalar.activation(y[h][:, u, :], z[h][:, u, :], ACT.Sigmoid)
+            nc.sync.dma_start(y_rows[:, :, cols], y[h][:])
+        for h in range(HALVES):
+            cols = slice(h * HALF, (h + 1) * HALF)
+            y_bf = keep.tile([P, HALF, PACK], BF16, name=f"y_bf{h}", align_bytes=64)
+            y_codes = keep.tile([P, HALF], I32, name=f"y_codes{h}", align_bytes=64)
+            nc.vector.tensor_copy(interleaved(y_bf[:]), by_rows(y[h][:]))
+            quantize(y_bf[:], y_codes[:], y_scales[:, cols])
+            nc.sync.dma_start(word_rows[:, cols], y_codes[:])
+        for quad in range(4):
+            queue = nc.scalar if quad % 2 == 0 else nc.sync
+            queue.dma_start(out_2[0, 4 * quad : 4 * quad + 4, :].bitcast(I32), y_scales[32 * quad : 32 * quad + 4, :].bitcast(I32))

@@ -40,70 +40,75 @@ def tile_attend_plw_quest_topk_kernel(tc, qT, k_words, k_scales, c_words, c_scal
         offsets = keep.tile([P, SLOTS // 16], U16, name="offsets")
         nc.sync.dma_start(offsets[:], offs)
 
-        ks_pool = keep.tile([P, PAGES], U8, name="ks_pool")
+        ks_pool = keep.tile([P, PAGES], U8, name="ks_pool", tag="ks_then_lo0", align_bytes=64)
         cs_pool = keep.tile([P, PAGES], U8, name="cs_pool")
         nc.vector.memset(ks_pool[:].bitcast(I32), 0)
-        nc.vector.memset(cs_pool[:].bitcast(I32), 0)
-        for quad in range(4):
-            nc.scalar.dma_start(ks_pool[32 * quad : 32 * quad + 4, :].bitcast(I32), k_scales[0, 4 * quad : 4 * quad + 4, :].bitcast(I32))
-        for quad in range(4):
-            nc.gpsimd.dma_start(cs_pool[32 * quad : 32 * quad + 4, :].bitcast(I32), c_scales[0, 4 * quad : 4 * quad + 4, :].bitcast(I32))
+        nc.gpsimd.memset(cs_pool[:].bitcast(I32), 0)
+
+        def load_scales(queue, pool, rows):
+            for quad in range(4):
+                queue.dma_start(pool[32 * quad : 32 * quad + 4, :].bitcast(I32), rows[0, 4 * quad : 4 * quad + 4, :].bitcast(I32))
+
+        q_rows = qT[0].rearrange("(p t) q -> p t q", t=PACK)
+        q_raw = [keep.tile([P, PACK, HALF], F32, name=f"q_raw{h}") for h in range(HALVES)]
+        k_pool = keep.tile([P, PAGES], I32, name="k_pool")
+        c_pool = keep.tile([P, PAGES], I32, name="c_pool")
         th_cols = keep.tile([P, PACK], F32, name="th_cols")
-        nc.gpsimd.dma_start(th_cols[:], th[0, 0, :].rearrange("(p c) -> p c", c=PACK))
+        k_rows = k_words[0].rearrange("p n t -> p (n t)").bitcast(I32)
+        nc.sync.dma_start(q_raw[0][:], q_rows[:, :, 0:HALF])
+        load_scales(nc.sync, ks_pool, k_scales)
+        nc.sync.dma_start(q_raw[1][:], q_rows[:, :, HALF:NQ])
+        nc.sync.dma_start(k_pool[:], k_rows)
+        nc.sync.dma_start(th_cols[:], th[0, 0, :].rearrange("(p c) -> p c", c=PACK))
+        load_scales(nc.sync, cs_pool, c_scales)
+        nc.sync.dma_start(c_pool[:], c_words[0].rearrange("p n t -> p (n t)").bitcast(I32))
 
         warm_in = keep.tile([P, 1], F32, name="warm_in")
         warm_out = keep.tile([P, 1], F32, name="warm_out")
         nc.vector.memset(warm_in[:], 0.0)
         nc.scalar.activation(warm_out[:], warm_in[:], ACT.Sigmoid)
 
-        q_rows = qT[0].rearrange("(p t) q -> p t q", t=PACK)
-        q_raw = []
-        for h in range(HALVES):
-            raw = keep.tile([P, PACK, HALF], F32, name=f"q_raw{h}", tag=f"stage{h}")
-            nc.sync.dma_start(raw[:], q_rows[:, :, h * HALF : (h + 1) * HALF])
-            q_raw.append(raw)
-        k_pool = keep.tile([P, PAGES], I32, name="k_pool")
-        nc.sync.dma_start(k_pool[:], k_words[0].rearrange("p n t -> p (n t)").bitcast(I32))
-
         def gather_scales(pool, name):
-            listed = keep.tile([P, SLOTS], U8, name=name + "_listed", tag=name + "_chain", align_bytes=64)
-            dealt = keep.tile([P, SLOTS], U8, name=name + "_dealt", align_bytes=64)
+            listed = keep.tile([P, SLOTS], U8, name=name)
             nc.vector.tensor_copy(listed[:], pool[:].indirect(offsets[:]))
+            return listed
+
+        def deal_scales(listed, name):
+            dealt = keep.tile([P, SLOTS], U8, name=name, align_bytes=64)
             nc.vector.tensor_copy(dealt[:].rearrange("p (t s) -> p t s", t=PACK), listed[:].rearrange("p (s t) -> p t s", t=PACK))
             return dealt
 
-        def gather_words(pool, name, tag):
-            dealt = keep.tile([P, SLOTS], U32, name=name, tag=tag, align_bytes=64)
+        def gather_words(pool, name):
+            dealt = keep.tile([P, SLOTS], U32, name=name, align_bytes=64)
             nc.vector.tensor_copy(dealt[:].rearrange("p (t s) -> p s t", t=PACK), pool[:].bitcast(U32).indirect(offsets[:]))
             return dealt
 
         def quantize(values, codes, scales):
             nc.vector.quantize_mx(out=codes.bitcast(FP8X4), scales=scales, in_=values.rearrange("p c t -> p (c t)"))
 
-        ks = gather_scales(ks_pool, "ks")
-        cs = gather_scales(cs_pool, "cs")
+        ks_listed = gather_scales(ks_pool, "ks_listed")
 
         q_bf = [keep.tile([P, HALF, PACK], BF16, name=f"q_bf{h}", align_bytes=64) for h in range(HALVES)]
-        hi = [keep.tile([P, HALF, PACK], BF16, name=f"hi{h}", tag=("hi0", "cs_chain")[h], align_bytes=64) for h in range(HALVES)]
-        lo = [keep.tile([P, HALF, PACK], BF16, name=f"lo{h}", align_bytes=64) for h in range(HALVES)]
+        hi = [keep.tile([P, HALF, PACK], BF16, name=f"hi{h}", align_bytes=64) for h in range(HALVES)]
+        lo = [keep.tile([P, HALF, PACK], BF16, name=f"lo{h}", tag=("ks_then_lo0", "lo1")[h], align_bytes=64) for h in range(HALVES)]
         hi_codes = [keep.tile([P, HALF], U32, name=f"hi_codes{h}", align_bytes=64) for h in range(HALVES)]
         lo_codes = [keep.tile([P, HALF], U32, name=f"lo_codes{h}", align_bytes=64) for h in range(HALVES)]
         hi_scales = [keep.tile([P, HALF], U8, name=f"hi_scales{h}", align_bytes=64) for h in range(HALVES)]
         lo_scales = [keep.tile([P, HALF], U8, name=f"lo_scales{h}", align_bytes=64) for h in range(HALVES)]
         for h in range(HALVES):
             nc.scalar.copy(interleaved(q_bf[h][:]), by_rows(q_raw[h][:]))
-        c_pool = keep.tile([P, PAGES], I32, name="c_pool", tag="stage0")
-        nc.sync.dma_start(c_pool[:], c_words[0].rearrange("p n t -> p (n t)").bitcast(I32))
         nc.scalar.activation(hi[0][:], q_bf[0][:], ACT.Relu)
         nc.vector.tensor_scalar_min(lo[0][:], q_bf[0][:], 0.0)
+        ks = deal_scales(ks_listed, "ks")
+        quantize(lo[0][:], lo_codes[0][:], lo_scales[0][:])
         nc.vector.tensor_scalar_max(hi[1][:], q_bf[1][:], 0.0)
         nc.vector.tensor_scalar_min(lo[1][:], q_bf[1][:], 0.0)
-        quantize(lo[0][:], lo_codes[0][:], lo_scales[0][:])
         quantize(hi[1][:], hi_codes[1][:], hi_scales[1][:])
-        quantize(hi[0][:], hi_codes[0][:], hi_scales[0][:])
-        kw = gather_words(k_pool, "kw", "cs_chain")
         quantize(lo[1][:], lo_codes[1][:], lo_scales[1][:])
-        cw = gather_words(c_pool, "cw", "cw")
+        quantize(hi[0][:], hi_codes[0][:], hi_scales[0][:])
+        kw = gather_words(k_pool, "kw")
+        cs = deal_scales(gather_scales(cs_pool, "cs_listed"), "cs")
+        cw = gather_words(c_pool, "cw")
 
         ident = keep.tile([P, P], F32, name="ident")
         make_identity(nc, ident[:])
@@ -142,14 +147,17 @@ def tile_attend_plw_quest_topk_kernel(tc, qT, k_words, k_scales, c_words, c_scal
             for u in range(PACK):
                 nc.vector.tensor_sub(z[h][:, u, :], banks[h][u][:], th_rows[:, cols])
                 nc.scalar.activation(y[h][:, u, :], z[h][:, u, :], ACT.Sigmoid)
-            nc.sync.dma_start(y_rows[:, :, cols], y[h][:])
+                if u % 2 == 1:
+                    nc.sync.dma_start(y_rows[:, u - 1 : u + 1, cols], y[h][:, u - 1 : u + 1, :])
+        y_bf = [keep.tile([P, HALF, PACK], BF16, name=f"y_bf{h}", align_bytes=64) for h in range(HALVES)]
+        y_codes = [keep.tile([P, HALF], I32, name=f"y_codes{h}", align_bytes=64) for h in range(HALVES)]
+        nc.vector.tensor_copy(interleaved(y_bf[0][:]), by_rows(y[0][:]))
+        nc.vector.tensor_copy(interleaved(y_bf[1][:, : HALF // 2, :]), by_rows(y[1][:, :, : HALF // 2]))
+        nc.scalar.copy(interleaved(y_bf[1][:, HALF // 2 :, :]), by_rows(y[1][:, :, HALF // 2 :]))
         for h in range(HALVES):
             cols = slice(h * HALF, (h + 1) * HALF)
-            y_bf = keep.tile([P, HALF, PACK], BF16, name=f"y_bf{h}", align_bytes=64)
-            y_codes = keep.tile([P, HALF], I32, name=f"y_codes{h}", align_bytes=64)
-            nc.vector.tensor_copy(interleaved(y_bf[:]), by_rows(y[h][:]))
-            quantize(y_bf[:], y_codes[:], y_scales[:, cols])
-            nc.sync.dma_start(word_rows[:, cols], y_codes[:])
+            quantize(y_bf[h][:], y_codes[h][:], y_scales[:, cols])
+            nc.sync.dma_start(word_rows[:, cols], y_codes[h][:])
         for quad in range(4):
             queue = nc.scalar if quad % 2 == 0 else nc.sync
             queue.dma_start(out_2[0, 4 * quad : 4 * quad + 4, :].bitcast(I32), y_scales[32 * quad : 32 * quad + 4, :].bitcast(I32))

@@ -20,6 +20,7 @@ SLOTS = 512
 NQ = 512
 HALVES = 2
 HALF = NQ // HALVES
+SPLIT = 160
 FLOPS = 2 * 2 * SLOTS * 512 * NQ
 
 
@@ -45,38 +46,30 @@ def tile_attend_plw_quest_topk_kernel(tc, qT, k_words, k_scales, c_words, c_scal
         nc.vector.memset(ks_pool[:].bitcast(I32), 0)
         nc.gpsimd.memset(cs_pool[:].bitcast(I32), 0)
 
-        def load_scales(queue, pool, rows):
+        def load_scales(pool, rows):
             for quad in range(4):
-                queue.dma_start(pool[32 * quad : 32 * quad + 4, :].bitcast(I32), rows[0, 4 * quad : 4 * quad + 4, :].bitcast(I32))
+                nc.sync.dma_start(pool[32 * quad : 32 * quad + 4, :].bitcast(I32), rows[0, 4 * quad : 4 * quad + 4, :].bitcast(I32))
 
         q_rows = qT[0].rearrange("(p t) q -> p t q", t=PACK)
-        q_raw = [keep.tile([P, PACK, HALF], F32, name=f"q_raw{h}") for h in range(HALVES)]
+        q_raw = [keep.tile([P, PACK, HALF], F32, name=f"q_raw{h}", tag=f"stage{h}", align_bytes=64) for h in range(HALVES)]
         k_pool = keep.tile([P, PAGES], I32, name="k_pool")
-        c_pool = keep.tile([P, PAGES], I32, name="c_pool")
+        c_pool = keep.tile([P, PAGES], I32, name="c_pool", tag="c_then_lo1", align_bytes=64)
         th_cols = keep.tile([P, PACK], F32, name="th_cols")
-        k_rows = k_words[0].rearrange("p n t -> p (n t)").bitcast(I32)
-        nc.sync.dma_start(q_raw[0][:], q_rows[:, :, 0:HALF])
-        load_scales(nc.sync, ks_pool, k_scales)
-        nc.sync.dma_start(q_raw[1][:], q_rows[:, :, HALF:NQ])
-        nc.sync.dma_start(k_pool[:], k_rows)
         nc.sync.dma_start(th_cols[:], th[0, 0, :].rearrange("(p c) -> p c", c=PACK))
-        load_scales(nc.sync, cs_pool, c_scales)
+        nc.sync.dma_start(q_raw[0][:], q_rows[:, :, 0:HALF])
+        load_scales(ks_pool, k_scales)
+        nc.sync.dma_start(q_raw[1][:], q_rows[:, :, HALF:NQ])
+        nc.sync.dma_start(k_pool[:], k_words[0].rearrange("p n t -> p (n t)").bitcast(I32))
+        load_scales(cs_pool, c_scales)
         nc.sync.dma_start(c_pool[:], c_words[0].rearrange("p n t -> p (n t)").bitcast(I32))
-
-        warm_in = keep.tile([P, 1], F32, name="warm_in")
-        warm_out = keep.tile([P, 1], F32, name="warm_out")
-        nc.vector.memset(warm_in[:], 0.0)
-        nc.scalar.activation(warm_out[:], warm_in[:], ACT.Sigmoid)
 
         def gather_scales(pool, name):
             listed = keep.tile([P, SLOTS], U8, name=name)
             nc.vector.tensor_copy(listed[:], pool[:].indirect(offsets[:]))
             return listed
 
-        def deal_scales(listed, name):
-            dealt = keep.tile([P, SLOTS], U8, name=name, align_bytes=64)
+        def deal_scales(listed, dealt):
             nc.vector.tensor_copy(dealt[:].rearrange("p (t s) -> p t s", t=PACK), listed[:].rearrange("p (s t) -> p t s", t=PACK))
-            return dealt
 
         def gather_words(pool, name):
             dealt = keep.tile([P, SLOTS], U32, name=name, align_bytes=64)
@@ -89,26 +82,38 @@ def tile_attend_plw_quest_topk_kernel(tc, qT, k_words, k_scales, c_words, c_scal
         ks_listed = gather_scales(ks_pool, "ks_listed")
 
         q_bf = [keep.tile([P, HALF, PACK], BF16, name=f"q_bf{h}", align_bytes=64) for h in range(HALVES)]
-        hi = [keep.tile([P, HALF, PACK], BF16, name=f"hi{h}", align_bytes=64) for h in range(HALVES)]
-        lo = [keep.tile([P, HALF, PACK], BF16, name=f"lo{h}", tag=("ks_then_lo0", "lo1")[h], align_bytes=64) for h in range(HALVES)]
         hi_codes = [keep.tile([P, HALF], U32, name=f"hi_codes{h}", align_bytes=64) for h in range(HALVES)]
-        lo_codes = [keep.tile([P, HALF], U32, name=f"lo_codes{h}", align_bytes=64) for h in range(HALVES)]
         hi_scales = [keep.tile([P, HALF], U8, name=f"hi_scales{h}", align_bytes=64) for h in range(HALVES)]
         lo_scales = [keep.tile([P, HALF], U8, name=f"lo_scales{h}", align_bytes=64) for h in range(HALVES)]
+        ks = keep.tile([P, SLOTS], U8, name="ks", align_bytes=64)
+        cs = keep.tile([P, SLOTS], U8, name="cs", align_bytes=64)
+
         for h in range(HALVES):
             nc.scalar.copy(interleaved(q_bf[h][:]), by_rows(q_raw[h][:]))
-        nc.scalar.activation(hi[0][:], q_bf[0][:], ACT.Relu)
+        hi = [
+            keep.tile([P, HALF, PACK], BF16, name="hi0", tag="stage1", align_bytes=64),
+            keep.tile([P, HALF, PACK], BF16, name="hi1", align_bytes=64),
+        ]
+        for h in range(HALVES):
+            nc.scalar.activation(hi[h][:], q_bf[h][:], ACT.Relu)
+        lo = [
+            keep.tile([P, HALF, PACK], BF16, name="lo0", tag="ks_then_lo0", align_bytes=64),
+            keep.tile([P, HALF, PACK], BF16, name="lo1", align_bytes=64),
+        ]
         nc.vector.tensor_scalar_min(lo[0][:], q_bf[0][:], 0.0)
-        ks = deal_scales(ks_listed, "ks")
-        quantize(lo[0][:], lo_codes[0][:], lo_scales[0][:])
-        nc.vector.tensor_scalar_max(hi[1][:], q_bf[1][:], 0.0)
+        deal_scales(ks_listed, ks)
+        lo_codes0 = keep.tile([P, HALF], U32, name="lo_codes0", align_bytes=64)
+        quantize(lo[0][:], lo_codes0[:], lo_scales[0][:])
         nc.vector.tensor_scalar_min(lo[1][:], q_bf[1][:], 0.0)
-        quantize(hi[1][:], hi_codes[1][:], hi_scales[1][:])
-        quantize(lo[1][:], lo_codes[1][:], lo_scales[1][:])
         quantize(hi[0][:], hi_codes[0][:], hi_scales[0][:])
         kw = gather_words(k_pool, "kw")
-        cs = deal_scales(gather_scales(cs_pool, "cs_listed"), "cs")
+        quantize(hi[1][:], hi_codes[1][:], hi_scales[1][:])
+        cs_listed = gather_scales(cs_pool, "cs_listed")
+        deal_scales(cs_listed, cs)
         cw = gather_words(c_pool, "cw")
+        lo_codes1 = keep.tile([P, HALF], U32, name="lo_codes1", tag="c_then_lo1", align_bytes=64)
+        quantize(lo[1][:], lo_codes1[:], lo_scales[1][:])
+        lo_codes = [lo_codes0, lo_codes1]
 
         ident = keep.tile([P, P], F32, name="ident")
         make_identity(nc, ident[:])
@@ -120,22 +125,24 @@ def tile_attend_plw_quest_topk_kernel(tc, qT, k_words, k_scales, c_words, c_scal
 
         banks = [[psum.tile([P, HALF], F32, name=f"acc{h}{u}", tag=f"bank{PACK * h + u}") for u in range(PACK)] for h in range(HALVES)]
 
-        def product(words, scales, codes, q_scales, first):
-            for h in range(HALVES):
-                for u in range(PACK):
-                    cols = slice(u * P, (u + 1) * P)
-                    nc.tensor.matmul_mx(
-                        out=banks[h][u][:],
-                        lhsT=words[:, cols].bitcast(FP8X4),
-                        lhsT_scale=scales[:, cols],
-                        rhs=codes[h][:].bitcast(FP8X4),
-                        rhs_scale=q_scales[h][:],
-                        start=first,
-                        stop=not first,
-                    )
+        def product(h, u, words, scales, codes, q_scales, first):
+            cols = slice(u * P, (u + 1) * P)
+            nc.tensor.matmul_mx(
+                out=banks[h][u][:],
+                lhsT=words[:, cols].bitcast(FP8X4),
+                lhsT_scale=scales[:, cols],
+                rhs=codes[h][:].bitcast(FP8X4),
+                rhs_scale=q_scales[h][:],
+                start=first,
+                stop=not first,
+            )
 
-        product(kw, ks, hi_codes, hi_scales, True)
-        product(cw, cs, lo_codes, lo_scales, False)
+        for h in range(HALVES):
+            for u in range(PACK):
+                product(h, u, kw, ks, hi_codes, hi_scales, True)
+        for h in range(HALVES):
+            for u in range(PACK):
+                product(h, u, cw, cs, lo_codes, lo_scales, False)
 
         y_rows = out_0.rearrange("(p u) q -> p u q", u=PACK)
         word_rows = out_1[0].rearrange("p q t -> p (q t)").bitcast(I32)
@@ -152,8 +159,8 @@ def tile_attend_plw_quest_topk_kernel(tc, qT, k_words, k_scales, c_words, c_scal
         y_bf = [keep.tile([P, HALF, PACK], BF16, name=f"y_bf{h}", align_bytes=64) for h in range(HALVES)]
         y_codes = [keep.tile([P, HALF], I32, name=f"y_codes{h}", align_bytes=64) for h in range(HALVES)]
         nc.vector.tensor_copy(interleaved(y_bf[0][:]), by_rows(y[0][:]))
-        nc.vector.tensor_copy(interleaved(y_bf[1][:, : HALF // 2, :]), by_rows(y[1][:, :, : HALF // 2]))
-        nc.scalar.copy(interleaved(y_bf[1][:, HALF // 2 :, :]), by_rows(y[1][:, :, HALF // 2 :]))
+        nc.vector.tensor_copy(interleaved(y_bf[1][:, : SPLIT, :]), by_rows(y[1][:, :, :SPLIT]))
+        nc.scalar.copy(interleaved(y_bf[1][:, SPLIT:, :]), by_rows(y[1][:, :, SPLIT:]))
         for h in range(HALVES):
             cols = slice(h * HALF, (h + 1) * HALF)
             quantize(y_bf[h][:], y_codes[h][:], y_scales[:, cols])

@@ -44,7 +44,10 @@ def tile_attend_plw_quest_topk_kernel(tc, qT, k_words, k_scales, c_words, c_scal
         ks_pool = keep.tile([P, PAGES], U8, name="ks_pool", tag="ks_then_lo0", align_bytes=64)
         cs_pool = keep.tile([P, PAGES], U8, name="cs_pool")
         nc.vector.memset(ks_pool[:].bitcast(I32), 0)
-        nc.gpsimd.memset(cs_pool[:].bitcast(I32), 0)
+        nc.vector.memset(cs_pool[:].bitcast(I32), 0)
+        ident = keep.tile([P, P], F32, name="ident")
+        nc.vector.memset(ident[:], 0.0)
+        make_identity(nc, ident[:], nomemset=True)
 
         def load_scales(pool, rows):
             for quad in range(4):
@@ -81,7 +84,7 @@ def tile_attend_plw_quest_topk_kernel(tc, qT, k_words, k_scales, c_words, c_scal
 
         ks_listed = gather_scales(ks_pool, "ks_listed")
 
-        q_bf = [keep.tile([P, HALF, PACK], BF16, name=f"q_bf{h}", align_bytes=64) for h in range(HALVES)]
+        q_bf = [keep.tile([P, HALF, PACK], BF16, name=f"q_bf{h}", tag=f"rounded{h}", align_bytes=64) for h in range(HALVES)]
         hi_codes = [keep.tile([P, HALF], U32, name=f"hi_codes{h}", align_bytes=64) for h in range(HALVES)]
         hi_scales = [keep.tile([P, HALF], U8, name=f"hi_scales{h}", align_bytes=64) for h in range(HALVES)]
         lo_scales = [keep.tile([P, HALF], U8, name=f"lo_scales{h}", align_bytes=64) for h in range(HALVES)]
@@ -115,12 +118,10 @@ def tile_attend_plw_quest_topk_kernel(tc, qT, k_words, k_scales, c_words, c_scal
         quantize(lo[1][:], lo_codes1[:], lo_scales[1][:])
         lo_codes = [lo_codes0, lo_codes1]
 
-        ident = keep.tile([P, P], F32, name="ident")
-        make_identity(nc, ident[:])
         th_bank = psum.tile([P, PACK, P], F32, name="th_bank", tag="bank7")
         for c in range(PACK):
             nc.tensor.transpose(th_bank[:, c, :], th_cols[:, c : c + 1].to_broadcast([P, P]), ident[:])
-        th_rows = keep.tile([P, NQ], F32, name="th_rows")
+        th_rows = keep.tile([P, NQ], F32, name="th_rows", tag="rounded1", align_bytes=64)
         nc.scalar.copy(th_rows[:].rearrange("p (n c) -> p n c", c=PACK), th_bank[:].rearrange("p c n -> p n c"))
 
         banks = [[psum.tile([P, HALF], F32, name=f"acc{h}{u}", tag=f"bank{PACK * h + u}") for u in range(PACK)] for h in range(HALVES)]

from contextlib import ExitStack

import concourse.mybir as mybir
from concourse.masks import make_identity

F32 = mybir.dt.float32
BF16 = mybir.dt.bfloat16
I32 = mybir.dt.int32
U32 = mybir.dt.uint32
U16 = mybir.dt.uint16
U8 = mybir.dt.uint8
FP8X4 = mybir.dt.float8_e4m3fn_x4
ALU = mybir.AluOpType
ACT = mybir.ActivationFunctionType

P = 128
PACK = 4
PAGES = 2048
SLOTS = 512
NQ = 512
HALVES = 2
HALF = NQ // HALVES
SPLIT = 160
FLOPS = 2 * 2 * SLOTS * 512 * NQ


def interleaved(dst):
    return dst.rearrange("p (c i) t -> p c t i", i=4)


def by_rows(src):
    return src.rearrange("p t (c i) -> p c t i", i=4)


def tile_attend_plw_quest_topk_kernel(tc, qT, k_words, k_scales, c_words, c_scales, th, offs, out_0, out_1, out_2):
    nc = tc.nc
    with ExitStack() as ctx:
        keep = ctx.enter_context(tc.tile_pool(name="keep", bufs=1))
        psum = ctx.enter_context(tc.psum_pool(name="psum", bufs=1))

        offsets = keep.tile([P, SLOTS // 16], U16, name="offsets")
        nc.sync.dma_start(offsets[:], offs)

        ks_pool = keep.tile([P, PAGES], U8, name="ks_pool", tag="ks_then_lo0", align_bytes=64)
        cs_pool = keep.tile([P, PAGES], U8, name="cs_pool")
        nc.vector.memset(ks_pool[:].bitcast(I32), 0)
        nc.vector.memset(cs_pool[:].bitcast(I32), 0)
        ident = keep.tile([P, P], F32, name="ident")
        nc.vector.memset(ident[:], 0.0)
        make_identity(nc, ident[:], nomemset=True)

        def load_scales(pool, rows):
            for quad in range(4):
                nc.sync.dma_start(pool[32 * quad : 32 * quad + 4, :].bitcast(I32), rows[0, 4 * quad : 4 * quad + 4, :].bitcast(I32))

        q_rows = qT[0].rearrange("(p t) q -> p t q", t=PACK)
        q_raw = [keep.tile([P, PACK, HALF], F32, name=f"q_raw{h}", tag=f"stage{h}", align_bytes=64) for h in range(HALVES)]
        k_pool = keep.tile([P, PAGES], I32, name="k_pool")
        c_pool = keep.tile([P, PAGES], I32, name="c_pool", tag="c_then_lo1", align_bytes=64)
        th_cols = keep.tile([P, PACK], F32, name="th_cols")
        nc.sync.dma_start(th_cols[:], th[0, 0, :].rearrange("(p c) -> p c", c=PACK))
        nc.sync.dma_start(q_raw[0][:], q_rows[:, :, 0:HALF])
        load_scales(ks_pool, k_scales)
        nc.sync.dma_start(q_raw[1][:], q_rows[:, :, HALF:NQ])
        nc.sync.dma_start(k_pool[:], k_words[0].rearrange("p n t -> p (n t)").bitcast(I32))
        load_scales(cs_pool, c_scales)
        nc.sync.dma_start(c_pool[:], c_words[0].rearrange("p n t -> p (n t)").bitcast(I32))

        def gather_scales(pool, name):
            listed = keep.tile([P, SLOTS], U8, name=name)
            nc.vector.tensor_copy(listed[:], pool[:].indirect(offsets[:]))
            return listed

        def deal_scales(listed, dealt):
            nc.vector.tensor_copy(dealt[:].rearrange("p (t s) -> p t s", t=PACK), listed[:].rearrange("p (s t) -> p t s", t=PACK))

        def gather_words(pool, name):
            dealt = keep.tile([P, SLOTS], U32, name=name, align_bytes=64)
            nc.vector.tensor_copy(dealt[:].rearrange("p (t s) -> p s t", t=PACK), pool[:].bitcast(U32).indirect(offsets[:]))
            return dealt

        def quantize(values, codes, scales):
            nc.vector.quantize_mx(out=codes.bitcast(FP8X4), scales=scales, in_=values.rearrange("p c t -> p (c t)"))

        ks_listed = gather_scales(ks_pool, "ks_listed")

        q_bf = [keep.tile([P, HALF, PACK], BF16, name=f"q_bf{h}", tag=f"rounded{h}", align_bytes=64) for h in range(HALVES)]
        hi_codes = [keep.tile([P, HALF], U32, name=f"hi_codes{h}", align_bytes=64) for h in range(HALVES)]
        hi_scales = [keep.tile([P, HALF], U8, name=f"hi_scales{h}", align_bytes=64) for h in range(HALVES)]
        lo_scales = [keep.tile([P, HALF], U8, name=f"lo_scales{h}", align_bytes=64) for h in range(HALVES)]
        ks = keep.tile([P, SLOTS], U8, name="ks", align_bytes=64)
        cs = keep.tile([P, SLOTS], U8, name="cs", align_bytes=64)

        for h in range(HALVES):
            nc.scalar.copy(interleaved(q_bf[h][:]), by_rows(q_raw[h][:]))
        hi = [
            keep.tile([P, HALF, PACK], BF16, name="hi0", tag="stage1", align_bytes=64),
            keep.tile([P, HALF, PACK], BF16, name="hi1", align_bytes=64),
        ]
        for h in range(HALVES):
            nc.scalar.activation(hi[h][:], q_bf[h][:], ACT.Relu)
        lo = [
            keep.tile([P, HALF, PACK], BF16, name="lo0", tag="ks_then_lo0", align_bytes=64),
            keep.tile([P, HALF, PACK], BF16, name="lo1", align_bytes=64),
        ]
        nc.vector.tensor_scalar_min(lo[0][:], q_bf[0][:], 0.0)
        deal_scales(ks_listed, ks)
        lo_codes0 = keep.tile([P, HALF], U32, name="lo_codes0", align_bytes=64)
        quantize(lo[0][:], lo_codes0[:], lo_scales[0][:])
        nc.vector.tensor_scalar_min(lo[1][:], q_bf[1][:], 0.0)
        quantize(hi[0][:], hi_codes[0][:], hi_scales[0][:])
        kw = gather_words(k_pool, "kw")
        quantize(hi[1][:], hi_codes[1][:], hi_scales[1][:])
        cs_listed = gather_scales(cs_pool, "cs_listed")
        deal_scales(cs_listed, cs)
        cw = gather_words(c_pool, "cw")
        lo_codes1 = keep.tile([P, HALF], U32, name="lo_codes1", tag="c_then_lo1", align_bytes=64)
        quantize(lo[1][:], lo_codes1[:], lo_scales[1][:])
        lo_codes = [lo_codes0, lo_codes1]

        th_bank = psum.tile([P, PACK, P], F32, name="th_bank", tag="bank7")
        for c in range(PACK):
            nc.tensor.transpose(th_bank[:, c, :], th_cols[:, c : c + 1].to_broadcast([P, P]), ident[:])
        th_rows = keep.tile([P, NQ], F32, name="th_rows", tag="rounded1", align_bytes=64)
        nc.scalar.copy(th_rows[:].rearrange("p (n c) -> p n c", c=PACK), th_bank[:].rearrange("p c n -> p n c"))

        banks = [[psum.tile([P, HALF], F32, name=f"acc{h}{u}", tag=f"bank{PACK * h + u}") for u in range(PACK)] for h in range(HALVES)]

        def product(h, u, words, scales, codes, q_scales, first):
            cols = slice(u * P, (u + 1) * P)
            nc.tensor.matmul_mx(
                out=banks[h][u][:],
                lhsT=words[:, cols].bitcast(FP8X4),
                lhsT_scale=scales[:, cols],
                rhs=codes[h][:].bitcast(FP8X4),
                rhs_scale=q_scales[h][:],
                start=first,
                stop=not first,
            )

        for h in range(HALVES):
            for u in range(PACK):
                product(h, u, kw, ks, hi_codes, hi_scales, True)
        for h in range(HALVES):
            for u in range(PACK):
                product(h, u, cw, cs, lo_codes, lo_scales, False)

        y_rows = out_0.rearrange("(p u) q -> p u q", u=PACK)
        word_rows = out_1[0].rearrange("p q t -> p (q t)").bitcast(I32)
        y_scales = keep.tile([P, NQ], U8, name="y_scales", align_bytes=64)
        z = [keep.tile([P, PACK, HALF], F32, name=f"z{h}") for h in range(HALVES)]
        y = [keep.tile([P, PACK, HALF], F32, name=f"y{h}") for h in range(HALVES)]
        for h in range(HALVES):
            cols = slice(h * HALF, (h + 1) * HALF)
            for u in range(PACK):
                nc.vector.tensor_sub(z[h][:, u, :], banks[h][u][:], th_rows[:, cols])
                nc.scalar.activation(y[h][:, u, :], z[h][:, u, :], ACT.Sigmoid)
                if u % 2 == 1:
                    nc.sync.dma_start(y_rows[:, u - 1 : u + 1, cols], y[h][:, u - 1 : u + 1, :])
        y_bf = [keep.tile([P, HALF, PACK], BF16, name=f"y_bf{h}", align_bytes=64) for h in range(HALVES)]
        y_codes = [keep.tile([P, HALF], I32, name=f"y_codes{h}", align_bytes=64) for h in range(HALVES)]
        nc.vector.tensor_copy(interleaved(y_bf[0][:]), by_rows(y[0][:]))
        nc.vector.tensor_copy(interleaved(y_bf[1][:, : SPLIT, :]), by_rows(y[1][:, :, :SPLIT]))
        nc.scalar.copy(interleaved(y_bf[1][:, SPLIT:, :]), by_rows(y[1][:, :, SPLIT:]))
        for h in range(HALVES):
            cols = slice(h * HALF, (h + 1) * HALF)
            quantize(y_bf[h][:], y_codes[h][:], y_scales[:, cols])
            nc.sync.dma_start(word_rows[:, cols], y_codes[h][:])
        for quad in range(4):
            queue = nc.scalar if quad % 2 == 0 else nc.sync
            queue.dma_start(out_2[0, 4 * quad : 4 * quad + 4, :].bitcast(I32), y_scales[32 * quad : 32 * quad + 4, :].bitcast(I32))
